import numpy as np
import ml_dtypes


def mxq(x, axis, fmt="e4m3"):
    dtype, down = {"e4m3": (ml_dtypes.float8_e4m3fn, 7), "e5m2": (ml_dtypes.float8_e5m2, 14)}[fmt]
    v = np.moveaxis(np.asarray(x, np.float32).astype(ml_dtypes.bfloat16).astype(np.float64), axis, -1)
    blocks = v.reshape(v.shape[:-1] + (-1, 32))
    amax = np.abs(blocks).max(-1, keepdims=True)
    byte = np.maximum(np.where(amax > 0, np.frexp(amax)[1] - 1 + 127, 0) - down, 1)
    scale = np.exp2(byte - 127.0)
    codes = (blocks / scale).astype(np.float32).astype(dtype).astype(np.float64)
    return np.moveaxis((codes * scale).reshape(v.shape), -1, axis)


WIDE = False


def mx_kscale(k):
    if not WIDE:
        return np.ones(k)
    levels = np.array([10, -10, 5, -5, 0])
    if k % 512:
        return np.exp2(np.random.permutation(np.resize(levels, k // 32))).repeat(32)
    a = np.empty((k // 512, 16))
    for p in range(k // 512):
        a[p, :8] = np.random.permutation(np.resize(levels, 8))
        for g in range(8):
            far = levels[np.abs(levels - a[p, g]) >= 10]
            a[p, g + 8] = far[np.random.randint(len(far))]
    return np.exp2(a.ravel()).repeat(32)


def f64(x):
    return np.asarray(x).astype(np.float64)


def striped(idx):
    return np.tile(idx.reshape(-1, 16).T, (8, 1)).astype(np.uint16)


def unstriped(offs):
    return offs[:16].T.reshape(-1).astype(np.int64)


def relu(v):
    return np.maximum(v, 0.0)


K, T, E, C, N = 1024, 512, 4, 256, 512


def by_expert(wq, xq):
    return np.concatenate([wq[e].T @ xq[:, e * C:(e + 1) * C] for e in range(E)], axis=1)


def setup_inputs():
    n = np.random.standard_normal
    s = mx_kscale(K)[:, None]
    first = np.random.permutation(np.repeat(np.arange(E), T // E))
    second = (first + 1 + np.random.permutation(np.repeat(np.arange(E - 1), -(-T // (E - 1)))[:T])) % E
    while np.bincount(second, minlength=E).max() != T // E:
        load = np.bincount(second, minlength=E); hi, lo = int(load.argmax()), int(load.argmin())
        t = np.flatnonzero((second == hi) & (first != lo))[0]; second[t] = lo
    slot_token = np.empty(E * C, np.int64); pos = np.empty((2, T), np.int64); fill = np.zeros(E, np.int64)
    place = np.stack([np.random.permutation(C) for _ in range(E)])
    for r, deal in enumerate((first, second)):
        for t in np.random.permutation(T):
            e = deal[t]; j = e * C + place[e, fill[e]]; fill[e] += 1; slot_token[j] = t; pos[r, t] = j
    g = np.random.uniform(0.2, 0.8, T)
    return {
        "xT": (n((K, T)) * s).astype(np.float32),
        "w": (n((E, K, N)) / np.sqrt(K) / s[None]).astype(np.float32),
        "b": (0.3 * n((N, E))).astype(np.float32),
        "gate": np.stack([np.tile(g, (N, 1)), np.tile(1.0 - g, (N, 1))]).astype(np.float32),
        "offs": striped(slot_token),
        "pos1": striped(pos[0]),
        "pos2": striped(pos[1]),
    }


def reference(xT, w, b, gate, offs, pos1, pos2):
    idx = unstriped(offs)
    xq = mxq(f64(xT)[:, idx], 0, "e4m3")
    y = by_expert(mxq(f64(w), 1, "e4m3"), xq)
    y = relu(y + np.repeat(f64(b), C, axis=1))
    return f64(gate[0]) * y[:, unstriped(pos1)] + f64(gate[1]) * y[:, unstriped(pos2)]

@@ -1,0 +1,121 @@
+from contextlib import ExitStack
+
+import concourse.mybir as mybir
+
+K, T, E, C, N = 1024, 512, 4, 256, 512
+FLOPS = 2 * E * C * K * N
+
+F32 = mybir.dt.float32
+BF16 = mybir.dt.bfloat16
+U32 = mybir.dt.uint32
+U16 = mybir.dt.uint16
+U8 = mybir.dt.uint8
+FP8X4 = mybir.dt.float8_e4m3fn_x4
+MULT = mybir.AluOpType.mult
+ADD = mybir.AluOpType.add
+RELU = mybir.ActivationFunctionType.Relu
+
+P = 128
+PACK = 4
+K_PASS = P * PACK
+PASSES = K // K_PASS
+NB = N // P
+
+
+def tile_routed_moe_kernel(tc, xT, w, b, gate, offs, pos1, pos2, out):
+    nc = tc.nc
+    with ExitStack() as ctx:
+        lists = ctx.enter_context(tc.tile_pool(name="lists", bufs=1))
+        keep = ctx.enter_context(tc.tile_pool(name="keep", bufs=1))
+        wraw_pool = ctx.enter_context(tc.tile_pool(name="wraw", bufs=8))
+        wb_pool = ctx.enter_context(tc.tile_pool(name="wb", bufs=3))
+        g4_pool = ctx.enter_context(tc.tile_pool(name="g4", bufs=4))
+        xb_pool = ctx.enter_context(tc.tile_pool(name="xb", bufs=3))
+        comb = ctx.enter_context(tc.tile_pool(name="comb", bufs=2))
+        psum = ctx.enter_context(tc.psum_pool(name="psum", bufs=8))
+
+        offs_t = lists.tile([P, E * C // 16], U16, name="offs_t")
+        nc.sync.dma_start(offs_t[:], offs)
+        pos1_t = lists.tile([P, T // 16], U16, name="pos1_t")
+        nc.sync.dma_start(pos1_t[:], pos1)
+        pos2_t = lists.tile([P, T // 16], U16, name="pos2_t")
+        nc.sync.dma_start(pos2_t[:], pos2)
+
+        x_view = xT.rearrange("(g p t) n -> g p t n", p=P, t=PACK)
+        planes = {}
+        for g in range(PASSES):
+            for t in range(PACK):
+                plane = keep.tile([P, T], F32, name="plane%d_%d" % (g, t))
+                nc.sync.dma_start(plane[:], x_view[g, :, t, :])
+                planes[(g, t)] = plane
+
+        b_t = keep.tile([P, NB, E], F32, name="b_t")
+        nc.sync.dma_start(b_t[:], b.rearrange("(nb p) e -> p nb e", p=P))
+
+        wraw = {}
+        for e in range(E):
+            for g in range(PASSES):
+                raw = wraw_pool.tile([P, PACK, N], F32, name="raw")
+                nc.sync.dma_start(
+                    raw[:], w[e, g * K_PASS : (g + 1) * K_PASS, :].rearrange("(p j) n -> p j n", j=PACK)
+                )
+                wraw[(e, g)] = raw
+
+        gates = {}
+        for nb in range(NB):
+            for r in range(2):
+                gt = keep.tile([P, T], F32, name="gate%d_%d" % (r, nb))
+                nc.sync.dma_start(gt[:], gate[r, nb * P : (nb + 1) * P, :])
+                gates[(r, nb)] = gt
+
+        y = [keep.tile([P, E * C], F32, name="y%d" % nb) for nb in range(NB)]
+
+        for e in range(E):
+            xc, xs, wc, ws = {}, {}, {}, {}
+            for g in range(PASSES):
+                g4 = g4_pool.tile([P, PACK, C], F32, name="g4")
+                for t in range(PACK):
+                    nc.vector.tensor_copy(
+                        out=g4[:, t, :],
+                        in_=planes[(g, t)][:].indirect(offs_t[:, e * (C // 16) : (e + 1) * (C // 16)]),
+                    )
+                xb = xb_pool.tile([P, C, PACK], BF16, name="xb", align_bytes=64)
+                nc.scalar.copy(out=xb[:], in_=g4[:].rearrange("p t n -> p n t"))
+                wb = wb_pool.tile([P, N, PACK], BF16, name="wb", align_bytes=64)
+                nc.scalar.copy(out=wb[:], in_=wraw[(e, g)][:].rearrange("p j n -> p n j"))
+
+                xc[g] = keep.tile([P, C], U32, name="xc%d_%d" % (e, g), align_bytes=64)
+                xs[g] = keep.tile([P, C], U8, name="xs%d_%d" % (e, g), align_bytes=64)
+                nc.vector.quantize_mx(
+                    out=xc[g][:].bitcast(FP8X4), scales=xs[g][:], in_=xb[:].rearrange("p n t -> p (n t)")
+                )
+                wc[g] = keep.tile([P, N], U32, name="wc%d_%d" % (e, g), align_bytes=64)
+                ws[g] = keep.tile([P, N], U8, name="ws%d_%d" % (e, g), align_bytes=64)
+                nc.vector.quantize_mx(
+                    out=wc[g][:].bitcast(FP8X4), scales=ws[g][:], in_=wb[:].rearrange("p n j -> p (n j)")
+                )
+
+            for nb in range(NB):
+                acc = psum.tile([P, C], F32, name="acc")
+                for g in range(PASSES):
+                    nc.tensor.matmul_mx(
+                        out=acc[:],
+                        lhsT=wc[g][:, nb * P : (nb + 1) * P].bitcast(FP8X4),
+                        lhsT_scale=ws[g][:, nb * P : (nb + 1) * P],
+                        rhs=xc[g][:].bitcast(FP8X4),
+                        rhs_scale=xs[g][:],
+                        start=(g == 0),
+                        stop=(g == PASSES - 1),
+                    )
+                nc.scalar.activation(
+                    out=y[nb][:, e * C : (e + 1) * C], in_=acc[:], func=RELU, bias=b_t[:, nb, e : e + 1]
+                )
+
+        for nb in range(NB):
+            t1 = comb.tile([P, T], F32, name="t1")
+            nc.vector.tensor_tensor(out=t1[:], in0=y[nb][:].indirect(pos1_t[:]), in1=gates[(0, nb)][:], op=MULT)
+            t2 = comb.tile([P, T], F32, name="t2")
+            nc.vector.tensor_tensor(out=t2[:], in0=y[nb][:].indirect(pos2_t[:]), in1=gates[(1, nb)][:], op=MULT)
+            res = comb.tile([P, T], F32, name="res")
+            nc.vector.tensor_tensor(out=res[:], in0=t1[:], in1=t2[:], op=ADD)
+            nc.sync.dma_start(out[nb * P : (nb + 1) * P, :], res[:])

@@ -20,6 +20,10 @@ PACK = 4
 K_PASS = P * PACK
 PASSES = K // K_PASS
 NB = N // P
+H = 2
+NH = N // H
+NBH = NB // H
+LC = C // 16
 
 
 def tile_routed_moe_kernel(tc, xT, w, b, gate, offs, pos1, pos2, out):
@@ -27,40 +31,38 @@ def tile_routed_moe_kernel(tc, xT, w, b, gate, offs, pos1, pos2, out):
     with ExitStack() as ctx:
         lists = ctx.enter_context(tc.tile_pool(name="lists", bufs=1))
         keep = ctx.enter_context(tc.tile_pool(name="keep", bufs=1))
-        wraw_pool = ctx.enter_context(tc.tile_pool(name="wraw", bufs=8))
-        wb_pool = ctx.enter_context(tc.tile_pool(name="wb", bufs=3))
-        g4_pool = ctx.enter_context(tc.tile_pool(name="g4", bufs=4))
-        xb_pool = ctx.enter_context(tc.tile_pool(name="xb", bufs=3))
         comb = ctx.enter_context(tc.tile_pool(name="comb", bufs=2))
         psum = ctx.enter_context(tc.psum_pool(name="psum", bufs=8))
 
         offs_t = lists.tile([P, E * C // 16], U16, name="offs_t")
         nc.sync.dma_start(offs_t[:], offs)
+
+        x_view = xT.rearrange("(g p t) n -> g p t n", p=P, t=PACK)
+        xr = []
+        for g in range(PASSES):
+            xr.append(keep.tile([P, PACK, T], F32, name="xr%d" % g))
+            for t in range(PACK):
+                nc.sync.dma_start(xr[g][:, t, :], x_view[g, :, t, :])
+
+        wraw = {}
+        for h in range(H):
+            for e in range(E):
+                raw = keep.tile([P, PASSES, PACK, NH], F32, name="raw%d_%d" % (e, h))
+                for g in range(PASSES):
+                    nc.sync.dma_start(
+                        raw[:, g],
+                        w[e, g * K_PASS : (g + 1) * K_PASS, h * NH : (h + 1) * NH].rearrange(
+                            "(p j) n -> p j n", j=PACK
+                        ),
+                    )
+                wraw[(e, h)] = raw
+
+        b_t = keep.tile([P, NB, E], F32, name="b_t")
+        nc.sync.dma_start(b_t[:], b.rearrange("(nb p) e -> p nb e", p=P))
         pos1_t = lists.tile([P, T // 16], U16, name="pos1_t")
         nc.sync.dma_start(pos1_t[:], pos1)
         pos2_t = lists.tile([P, T // 16], U16, name="pos2_t")
         nc.sync.dma_start(pos2_t[:], pos2)
-
-        x_view = xT.rearrange("(g p t) n -> g p t n", p=P, t=PACK)
-        planes = {}
-        for g in range(PASSES):
-            for t in range(PACK):
-                plane = keep.tile([P, T], F32, name="plane%d_%d" % (g, t))
-                nc.sync.dma_start(plane[:], x_view[g, :, t, :])
-                planes[(g, t)] = plane
-
-        b_t = keep.tile([P, NB, E], F32, name="b_t")
-        nc.sync.dma_start(b_t[:], b.rearrange("(nb p) e -> p nb e", p=P))
-
-        wraw = {}
-        for e in range(E):
-            for g in range(PASSES):
-                raw = wraw_pool.tile([P, PACK, N], F32, name="raw")
-                nc.sync.dma_start(
-                    raw[:], w[e, g * K_PASS : (g + 1) * K_PASS, :].rearrange("(p j) n -> p j n", j=PACK)
-                )
-                wraw[(e, g)] = raw
-
         gates = {}
         for nb in range(NB):
             for r in range(2):
@@ -69,41 +71,45 @@ def tile_routed_moe_kernel(tc, xT, w, b, gate, offs, pos1, pos2, out):
                 gates[(r, nb)] = gt
 
         y = [keep.tile([P, E * C], F32, name="y%d" % nb) for nb in range(NB)]
+        xc, xs, wc, ws = {}, {}, {}, {}
 
-        for e in range(E):
-            xc, xs, wc, ws = {}, {}, {}, {}
+        def x_unit(e):
+            xb = keep.tile([P, PASSES, C, PACK], BF16, name="xb%d" % e, align_bytes=64)
             for g in range(PASSES):
-                g4 = g4_pool.tile([P, PACK, C], F32, name="g4")
                 for t in range(PACK):
                     nc.vector.tensor_copy(
-                        out=g4[:, t, :],
-                        in_=planes[(g, t)][:].indirect(offs_t[:, e * (C // 16) : (e + 1) * (C // 16)]),
+                        out=xb[:, g, :, t],
+                        in_=xr[g][:, t, :].indirect(offs_t[:, e * LC : (e + 1) * LC]),
                     )
-                xb = xb_pool.tile([P, C, PACK], BF16, name="xb", align_bytes=64)
-                nc.scalar.copy(out=xb[:], in_=g4[:].rearrange("p t n -> p n t"))
-                wb = wb_pool.tile([P, N, PACK], BF16, name="wb", align_bytes=64)
-                nc.scalar.copy(out=wb[:], in_=wraw[(e, g)][:].rearrange("p j n -> p n j"))
+            xc[e] = keep.tile([P, PASSES * C], U32, name="xc%d" % e, align_bytes=64)
+            xs[e] = keep.tile([P, PASSES * C], U8, name="xs%d" % e, align_bytes=64)
+            nc.vector.quantize_mx(
+                out=xc[e][:].bitcast(FP8X4), scales=xs[e][:], in_=xb[:].rearrange("p g n t -> p (g n t)")
+            )
 
-                xc[g] = keep.tile([P, C], U32, name="xc%d_%d" % (e, g), align_bytes=64)
-                xs[g] = keep.tile([P, C], U8, name="xs%d_%d" % (e, g), align_bytes=64)
-                nc.vector.quantize_mx(
-                    out=xc[g][:].bitcast(FP8X4), scales=xs[g][:], in_=xb[:].rearrange("p n t -> p (n t)")
-                )
-                wc[g] = keep.tile([P, N], U32, name="wc%d_%d" % (e, g), align_bytes=64)
-                ws[g] = keep.tile([P, N], U8, name="ws%d_%d" % (e, g), align_bytes=64)
-                nc.vector.quantize_mx(
-                    out=wc[g][:].bitcast(FP8X4), scales=ws[g][:], in_=wb[:].rearrange("p n j -> p (n j)")
-                )
+        def w_unit(e, h):
+            wb = keep.tile([P, PASSES, NH, PACK], BF16, name="wb%d_%d" % (e, h), align_bytes=64)
+            nc.scalar.copy(out=wb[:], in_=wraw[(e, h)][:].rearrange("p g j n -> p g n j"))
+            wc[(e, h)] = keep.tile([P, PASSES * NH], U32, name="wc%d_%d" % (e, h), align_bytes=64)
+            ws[(e, h)] = keep.tile([P, PASSES * NH], U8, name="ws%d_%d" % (e, h), align_bytes=64)
+            nc.vector.quantize_mx(
+                out=wc[(e, h)][:].bitcast(FP8X4),
+                scales=ws[(e, h)][:],
+                in_=wb[:].rearrange("p g n j -> p (g n j)"),
+            )
 
-            for nb in range(NB):
+        def multiply(e, h):
+            for i in range(NBH):
+                nb = h * NBH + i
                 acc = psum.tile([P, C], F32, name="acc")
                 for g in range(PASSES):
+                    cols = slice(g * NH + i * P, g * NH + (i + 1) * P)
                     nc.tensor.matmul_mx(
                         out=acc[:],
-                        lhsT=wc[g][:, nb * P : (nb + 1) * P].bitcast(FP8X4),
-                        lhsT_scale=ws[g][:, nb * P : (nb + 1) * P],
-                        rhs=xc[g][:].bitcast(FP8X4),
-                        rhs_scale=xs[g][:],
+                        lhsT=wc[(e, h)][:, cols].bitcast(FP8X4),
+                        lhsT_scale=ws[(e, h)][:, cols],
+                        rhs=xc[e][:, g * C : (g + 1) * C].bitcast(FP8X4),
+                        rhs_scale=xs[e][:, g * C : (g + 1) * C],
                         start=(g == 0),
                         stop=(g == PASSES - 1),
                     )
@@ -111,7 +117,7 @@ def tile_routed_moe_kernel(tc, xT, w, b, gate, offs, pos1, pos2, out):
                     out=y[nb][:, e * C : (e + 1) * C], in_=acc[:], func=RELU, bias=b_t[:, nb, e : e + 1]
                 )
 
-        for nb in range(NB):
+        def combine(nb):
             t1 = comb.tile([P, T], F32, name="t1")
             nc.vector.tensor_tensor(out=t1[:], in0=y[nb][:].indirect(pos1_t[:]), in1=gates[(0, nb)][:], op=MULT)
             t2 = comb.tile([P, T], F32, name="t2")
@@ -119,3 +125,14 @@ def tile_routed_moe_kernel(tc, xT, w, b, gate, offs, pos1, pos2, out):
             res = comb.tile([P, T], F32, name="res")
             nc.vector.tensor_tensor(out=res[:], in0=t1[:], in1=t2[:], op=ADD)
             nc.sync.dma_start(out[nb * P : (nb + 1) * P, :], res[:])
+
+        for e in range(E):
+            x_unit(e)
+        for h in range(H):
+            for e in range(E):
+                w_unit(e, h)
+        for h in range(H):
+            for e in range(E):
+                multiply(e, h)
+            for nb in range(h * NBH, (h + 1) * NBH):
+                combine(nb)

@@ -71,21 +71,29 @@ def tile_routed_moe_kernel(tc, xT, w, b, gate, offs, pos1, pos2, out):
                 gates[(r, nb)] = gt
 
         y = [keep.tile([P, E * C], F32, name="y%d" % nb) for nb in range(NB)]
-        xc, xs, wc, ws = {}, {}, {}, {}
+        pr, xb, xc, xs, wc, ws = {}, {}, {}, {}, {}, {}
 
-        def x_unit(e):
-            xb = keep.tile([P, PASSES, C, PACK], BF16, name="xb%d" % e, align_bytes=64)
+        def x_gather(e):
+            pr[e] = keep.tile([P, PASSES * C * PACK], BF16, name="pr%d" % e, align_bytes=64)
+            view = pr[e][:].rearrange("p (g u n i) -> p g u n i", g=PASSES, u=2, i=2)
             for g in range(PASSES):
                 for t in range(PACK):
                     nc.vector.tensor_copy(
-                        out=xb[:, g, :, t],
+                        out=view[:, g, t // 2, :, t % 2],
                         in_=xr[g][:, t, :].indirect(offs_t[:, e * LC : (e + 1) * LC]),
                     )
+
+        def x_words(e):
+            xb[e] = keep.tile([P, PASSES * C * PACK], BF16, name="xb%d" % e, align_bytes=64)
+            nc.vector.tensor_copy(
+                out=xb[e][:].bitcast(F32).rearrange("p (g n u) -> p g n u", g=PASSES, u=2),
+                in_=pr[e][:].bitcast(F32).rearrange("p (g u n) -> p g n u", g=PASSES, u=2),
+            )
+
+        def x_quant(e):
             xc[e] = keep.tile([P, PASSES * C], U32, name="xc%d" % e, align_bytes=64)
             xs[e] = keep.tile([P, PASSES * C], U8, name="xs%d" % e, align_bytes=64)
-            nc.vector.quantize_mx(
-                out=xc[e][:].bitcast(FP8X4), scales=xs[e][:], in_=xb[:].rearrange("p g n t -> p (g n t)")
-            )
+            nc.vector.quantize_mx(out=xc[e][:].bitcast(FP8X4), scales=xs[e][:], in_=xb[e][:])
 
         def w_unit(e, h):
             wb = keep.tile([P, PASSES, NH, PACK], BF16, name="wb%d_%d" % (e, h), align_bytes=64)
@@ -126,11 +134,24 @@ def tile_routed_moe_kernel(tc, xT, w, b, gate, offs, pos1, pos2, out):
             nc.vector.tensor_tensor(out=res[:], in0=t1[:], in1=t2[:], op=ADD)
             nc.sync.dma_start(out[nb * P : (nb + 1) * P, :], res[:])
 
+        x_gather(0)
+        x_gather(1)
+        x_words(0)
+        x_gather(2)
+        x_quant(0)
+        x_words(1)
+        x_gather(3)
+        x_quant(1)
+        x_words(2)
+        w_unit(0, 0)
+        x_quant(2)
+        x_words(3)
+        w_unit(1, 0)
+        x_quant(3)
+        w_unit(2, 0)
+        w_unit(3, 0)
         for e in range(E):
-            x_unit(e)
-        for h in range(H):
-            for e in range(E):
-                w_unit(e, h)
+            w_unit(e, 1)
         for h in range(H):
             for e in range(E):
                 multiply(e, h)

@@ -24,6 +24,9 @@ H = 2
 NH = N // H
 NBH = NB // H
 LC = C // 16
+COPY = mybir.ActivationFunctionType.Copy
+S_EXPERTS = (3, 2)
+G_UNITS = ((0, 0), (1, 0))
 
 
 def tile_routed_moe_kernel(tc, xT, w, b, gate, offs, pos1, pos2, out):
@@ -71,23 +74,43 @@ def tile_routed_moe_kernel(tc, xT, w, b, gate, offs, pos1, pos2, out):
                 gates[(r, nb)] = gt
 
         y = [keep.tile([P, E * C], F32, name="y%d" % nb) for nb in range(NB)]
+        UNIT = C * PACK
         pr, xb, xc, xs, wc, ws = {}, {}, {}, {}, {}, {}
+        for e in range(E):
+            xb[e] = keep.tile([P, PASSES * UNIT], BF16, name="xb%d" % e, align_bytes=64)
+
+        def v_passes(e):
+            return [g for g in range(PASSES) if not (g == 0 and e in S_EXPERTS)]
+
+        xbf = keep.tile([P, PACK, T], BF16, name="xbf")
+        for t in range(PACK):
+            nc.scalar.copy(out=xbf[:, t, :], in_=xr[0][:, t, :])
+        for e in S_EXPERTS:
+            place = xb[e][:, 0:UNIT].rearrange("p (n t) -> p n t", t=PACK)
+            for t in range(PACK):
+                nc.scalar.activation(
+                    out=place[:, :, t],
+                    in_=xbf[:, t, :].indirect(offs_t[:, e * LC : (e + 1) * LC]),
+                    func=COPY,
+                )
 
         def x_gather(e):
-            pr[e] = keep.tile([P, PASSES * C * PACK], BF16, name="pr%d" % e, align_bytes=64)
-            view = pr[e][:].rearrange("p (g u n i) -> p g u n i", g=PASSES, u=2, i=2)
-            for g in range(PASSES):
+            gs = v_passes(e)
+            pr[e] = keep.tile([P, len(gs) * UNIT], BF16, name="pr%d" % e, align_bytes=64)
+            view = pr[e][:].rearrange("p (a u n i) -> p a u n i", a=len(gs), u=2, i=2)
+            for a, g in enumerate(gs):
                 for t in range(PACK):
                     nc.vector.tensor_copy(
-                        out=view[:, g, t // 2, :, t % 2],
+                        out=view[:, a, t // 2, :, t % 2],
                         in_=xr[g][:, t, :].indirect(offs_t[:, e * LC : (e + 1) * LC]),
                     )
 
         def x_words(e):
-            xb[e] = keep.tile([P, PASSES * C * PACK], BF16, name="xb%d" % e, align_bytes=64)
+            gs = v_passes(e)
+            first = gs[0] * UNIT // 2
             nc.vector.tensor_copy(
-                out=xb[e][:].bitcast(F32).rearrange("p (g n u) -> p g n u", g=PASSES, u=2),
-                in_=pr[e][:].bitcast(F32).rearrange("p (g u n) -> p g n u", g=PASSES, u=2),
+                out=xb[e][:].bitcast(F32)[:, first:].rearrange("p (a n u) -> p a n u", a=len(gs), u=2),
+                in_=pr[e][:].bitcast(F32).rearrange("p (a u n) -> p a n u", a=len(gs), u=2),
             )
 
         def x_quant(e):
@@ -97,7 +120,18 @@ def tile_routed_moe_kernel(tc, xT, w, b, gate, offs, pos1, pos2, out):
 
         def w_unit(e, h):
             wb = keep.tile([P, PASSES, NH, PACK], BF16, name="wb%d_%d" % (e, h), align_bytes=64)
-            nc.scalar.copy(out=wb[:], in_=wraw[(e, h)][:].rearrange("p g j n -> p g n j"))
+            if (e, h) in G_UNITS:
+                for g in range(PASSES):
+                    nc.gpsimd.tensor_scalar(
+                        out=wb[:, g],
+                        in0=wraw[(e, h)][:, g].rearrange("p j n -> p n j"),
+                        scalar1=1.0,
+                        scalar2=0.0,
+                        op0=MULT,
+                        op1=ADD,
+                    )
+            else:
+                nc.scalar.copy(out=wb[:], in_=wraw[(e, h)][:].rearrange("p g j n -> p g n j"))
             wc[(e, h)] = keep.tile([P, PASSES * NH], U32, name="wc%d_%d" % (e, h), align_bytes=64)
             ws[(e, h)] = keep.tile([P, PASSES * NH], U8, name="ws%d_%d" % (e, h), align_bytes=64)
             nc.vector.quantize_mx(
@@ -134,26 +168,29 @@ def tile_routed_moe_kernel(tc, xT, w, b, gate, offs, pos1, pos2, out):
             nc.vector.tensor_tensor(out=res[:], in0=t1[:], in1=t2[:], op=ADD)
             nc.sync.dma_start(out[nb * P : (nb + 1) * P, :], res[:])
 
-        x_gather(0)
-        x_gather(1)
+        for e in range(E):
+            x_gather(e)
         x_words(0)
-        x_gather(2)
-        x_quant(0)
         x_words(1)
-        x_gather(3)
-        x_quant(1)
+        x_quant(0)
         x_words(2)
-        w_unit(0, 0)
-        x_quant(2)
+        x_quant(1)
         x_words(3)
-        w_unit(1, 0)
+        x_quant(2)
+        w_unit(0, 0)
         x_quant(3)
+        w_unit(1, 0)
         w_unit(2, 0)
         w_unit(3, 0)
+        w_unit(0, 1)
+        w_unit(1, 1)
+        w_unit(2, 1)
         for e in range(E):
-            w_unit(e, 1)
-        for h in range(H):
-            for e in range(E):
-                multiply(e, h)
-            for nb in range(h * NBH, (h + 1) * NBH):
-                combine(nb)
+            multiply(e, 0)
+        w_unit(3, 1)
+        combine(0)
+        combine(1)
+        for e in range(E):
+            multiply(e, 1)
+        combine(2)
+        combine(3)

@@ -26,7 +26,7 @@ NBH = NB // H
 LC = C // 16
 COPY = mybir.ActivationFunctionType.Copy
 S_EXPERTS = (3, 2)
-G_UNITS = ((0, 0), (1, 0))
+G_UNITS = ((0, 0), (1, 0), (2, 0), (3, 0))
 
 
 def tile_routed_moe_kernel(tc, xT, w, b, gate, offs, pos1, pos2, out):

@@ -25,7 +25,9 @@ NH = N // H
 NBH = NB // H
 LC = C // 16
 COPY = mybir.ActivationFunctionType.Copy
-S_EXPERTS = (3, 2)
+S_EXPERTS = (0, 1, 2, 3)
+B_AFTER = (1, 1)
+V_UNITS = ((2, 1), (3, 1))
 G_UNITS = ((0, 0), (1, 0), (2, 0), (3, 0))
 
 
@@ -41,13 +43,19 @@ def tile_routed_moe_kernel(tc, xT, w, b, gate, offs, pos1, pos2, out):
         nc.sync.dma_start(offs_t[:], offs)
 
         x_view = xT.rearrange("(g p t) n -> g p t n", p=P, t=PACK)
-        xr = []
-        for g in range(PASSES):
-            xr.append(keep.tile([P, PACK, T], F32, name="xr%d" % g))
-            for t in range(PACK):
+        xr = [keep.tile([P, PACK, T], F32, name="xr%d" % g) for g in range(PASSES)]
+        for t in range(PACK):
+            for g in range(PASSES):
                 nc.sync.dma_start(xr[g][:, t, :], x_view[g, :, t, :])
 
+        pos1_t = lists.tile([P, T // 16], U16, name="pos1_t")
+        nc.sync.dma_start(pos1_t[:], pos1)
+        pos2_t = lists.tile([P, T // 16], U16, name="pos2_t")
+        nc.sync.dma_start(pos2_t[:], pos2)
+
         wraw = {}
+        gates = {}
+        b_t = keep.tile([P, NB, E], F32, name="b_t")
         for h in range(H):
             for e in range(E):
                 raw = keep.tile([P, PASSES, PACK, NH], F32, name="raw%d_%d" % (e, h))
@@ -59,19 +67,13 @@ def tile_routed_moe_kernel(tc, xT, w, b, gate, offs, pos1, pos2, out):
                         ),
                     )
                 wraw[(e, h)] = raw
-
-        b_t = keep.tile([P, NB, E], F32, name="b_t")
-        nc.sync.dma_start(b_t[:], b.rearrange("(nb p) e -> p nb e", p=P))
-        pos1_t = lists.tile([P, T // 16], U16, name="pos1_t")
-        nc.sync.dma_start(pos1_t[:], pos1)
-        pos2_t = lists.tile([P, T // 16], U16, name="pos2_t")
-        nc.sync.dma_start(pos2_t[:], pos2)
-        gates = {}
-        for nb in range(NB):
-            for r in range(2):
-                gt = keep.tile([P, T], F32, name="gate%d_%d" % (r, nb))
-                nc.sync.dma_start(gt[:], gate[r, nb * P : (nb + 1) * P, :])
-                gates[(r, nb)] = gt
+                if (e, h) == B_AFTER:
+                    nc.sync.dma_start(b_t[:], b.rearrange("(nb p) e -> p nb e", p=P))
+            for nb in range(h * NBH, (h + 1) * NBH):
+                for r in range(2):
+                    gt = keep.tile([P, T], F32, name="gate%d_%d" % (r, nb))
+                    nc.sync.dma_start(gt[:], gate[r, nb * P : (nb + 1) * P, :])
+                    gates[(r, nb)] = gt
 
         y = [keep.tile([P, E * C], F32, name="y%d" % nb) for nb in range(NB)]
         UNIT = C * PACK
@@ -130,6 +132,8 @@ def tile_routed_moe_kernel(tc, xT, w, b, gate, offs, pos1, pos2, out):
                         op0=MULT,
                         op1=ADD,
                     )
+            elif (e, h) in V_UNITS:
+                nc.vector.tensor_copy(out=wb[:], in_=wraw[(e, h)][:].rearrange("p g j n -> p g n j"))
             else:
                 nc.scalar.copy(out=wb[:], in_=wraw[(e, h)][:].rearrange("p g j n -> p g n j"))
             wc[(e, h)] = keep.tile([P, PASSES * NH], U32, name="wc%d_%d" % (e, h), align_bytes=64)
@@ -174,13 +178,13 @@ def tile_routed_moe_kernel(tc, xT, w, b, gate, offs, pos1, pos2, out):
         x_words(1)
         x_quant(0)
         x_words(2)
-        x_quant(1)
-        x_words(3)
-        x_quant(2)
         w_unit(0, 0)
-        x_quant(3)
+        x_words(3)
+        x_quant(1)
         w_unit(1, 0)
+        x_quant(2)
         w_unit(2, 0)
+        x_quant(3)
         w_unit(3, 0)
         w_unit(0, 1)
         w_unit(1, 1)

@@ -14,21 +14,20 @@ FP8X4 = mybir.dt.float8_e4m3fn_x4
 MULT = mybir.AluOpType.mult
 ADD = mybir.AluOpType.add
 RELU = mybir.ActivationFunctionType.Relu
+COPY = mybir.ActivationFunctionType.Copy
 
 P = 128
 PACK = 4
 K_PASS = P * PACK
 PASSES = K // K_PASS
 NB = N // P
-H = 2
-NH = N // H
-NBH = NB // H
 LC = C // 16
-COPY = mybir.ActivationFunctionType.Copy
-S_EXPERTS = (0, 1, 2, 3)
-B_AFTER = (1, 1)
-V_UNITS = ((2, 1), (3, 1))
-G_UNITS = ((0, 0), (1, 0), (2, 0), (3, 0))
+UNIT = C * PACK
+S_EXPERTS = (3, 2, 1)
+W_ENGINE = {
+    (0, 0): "gpsimd", (0, 1): "scalar", (1, 0): "gpsimd", (1, 1): "scalar",
+    (2, 0): "gpsimd", (2, 1): "scalar", (3, 0): "scalar", (3, 1): "vector",
+}
 
 
 def tile_routed_moe_kernel(tc, xT, w, b, gate, offs, pos1, pos2, out):
@@ -44,45 +43,35 @@ def tile_routed_moe_kernel(tc, xT, w, b, gate, offs, pos1, pos2, out):
 
         x_view = xT.rearrange("(g p t) n -> g p t n", p=P, t=PACK)
         xr = [keep.tile([P, PACK, T], F32, name="xr%d" % g) for g in range(PASSES)]
-        for t in range(PACK):
-            for g in range(PASSES):
+        for g in range(PASSES):
+            for t in range(PACK):
                 nc.sync.dma_start(xr[g][:, t, :], x_view[g, :, t, :])
 
         pos1_t = lists.tile([P, T // 16], U16, name="pos1_t")
         nc.sync.dma_start(pos1_t[:], pos1)
         pos2_t = lists.tile([P, T // 16], U16, name="pos2_t")
         nc.sync.dma_start(pos2_t[:], pos2)
+        b_t = keep.tile([P, NB, E], F32, name="b_t")
 
         wraw = {}
-        gates = {}
-        b_t = keep.tile([P, NB, E], F32, name="b_t")
-        for h in range(H):
-            for e in range(E):
-                raw = keep.tile([P, PASSES, PACK, NH], F32, name="raw%d_%d" % (e, h))
-                for g in range(PASSES):
-                    nc.sync.dma_start(
-                        raw[:, g],
-                        w[e, g * K_PASS : (g + 1) * K_PASS, h * NH : (h + 1) * NH].rearrange(
-                            "(p j) n -> p j n", j=PACK
-                        ),
-                    )
-                wraw[(e, h)] = raw
-                if (e, h) == B_AFTER:
+        for e in range(E):
+            for g in range(PASSES):
+                wraw[(e, g)] = keep.tile([P, PACK, N], F32, name="raw%d_%d" % (e, g))
+                nc.sync.dma_start(
+                    wraw[(e, g)][:], w[e, g * K_PASS : (g + 1) * K_PASS, :].rearrange("(p j) n -> p j n", j=PACK)
+                )
+                if (e, g) == (3, 0):
                     nc.sync.dma_start(b_t[:], b.rearrange("(nb p) e -> p nb e", p=P))
-            for nb in range(h * NBH, (h + 1) * NBH):
-                for r in range(2):
-                    gt = keep.tile([P, T], F32, name="gate%d_%d" % (r, nb))
-                    nc.sync.dma_start(gt[:], gate[r, nb * P : (nb + 1) * P, :])
-                    gates[(r, nb)] = gt
+        gates = {}
+        for nb in range(NB):
+            for r in range(2):
+                gates[(r, nb)] = keep.tile([P, T], F32, name="gate%d_%d" % (r, nb))
+                nc.sync.dma_start(gates[(r, nb)][:], gate[r, nb * P : (nb + 1) * P, :])
 
         y = [keep.tile([P, E * C], F32, name="y%d" % nb) for nb in range(NB)]
-        UNIT = C * PACK
         pr, xb, xc, xs, wc, ws = {}, {}, {}, {}, {}, {}
         for e in range(E):
             xb[e] = keep.tile([P, PASSES * UNIT], BF16, name="xb%d" % e, align_bytes=64)
-
-        def v_passes(e):
-            return [g for g in range(PASSES) if not (g == 0 and e in S_EXPERTS)]
 
         xbf = keep.tile([P, PACK, T], BF16, name="xbf")
         for t in range(PACK):
@@ -95,6 +84,9 @@ def tile_routed_moe_kernel(tc, xT, w, b, gate, offs, pos1, pos2, out):
                     in_=xbf[:, t, :].indirect(offs_t[:, e * LC : (e + 1) * LC]),
                     func=COPY,
                 )
+
+        def v_passes(e):
+            return [g for g in range(PASSES) if not (g == 0 and e in S_EXPERTS)]
 
         def x_gather(e):
             gs = v_passes(e)
@@ -120,40 +112,34 @@ def tile_routed_moe_kernel(tc, xT, w, b, gate, offs, pos1, pos2, out):
             xs[e] = keep.tile([P, PASSES * C], U8, name="xs%d" % e, align_bytes=64)
             nc.vector.quantize_mx(out=xc[e][:].bitcast(FP8X4), scales=xs[e][:], in_=xb[e][:])
 
-        def w_unit(e, h):
-            wb = keep.tile([P, PASSES, NH, PACK], BF16, name="wb%d_%d" % (e, h), align_bytes=64)
-            if (e, h) in G_UNITS:
-                for g in range(PASSES):
+        def w_piece(e, g):
+            wb = keep.tile([P, N, PACK], BF16, name="wb%d_%d" % (e, g), align_bytes=64)
+            src = wraw[(e, g)][:].rearrange("p j n -> p n j")
+            if W_ENGINE[(e, g)] == "gpsimd":
+                for half in range(2):
+                    cols = slice(half * N // 2, (half + 1) * N // 2)
                     nc.gpsimd.tensor_scalar(
-                        out=wb[:, g],
-                        in0=wraw[(e, h)][:, g].rearrange("p j n -> p n j"),
-                        scalar1=1.0,
-                        scalar2=0.0,
-                        op0=MULT,
-                        op1=ADD,
+                        out=wb[:, cols, :], in0=src[:, cols, :], scalar1=1.0, scalar2=0.0, op0=MULT, op1=ADD
                     )
-            elif (e, h) in V_UNITS:
-                nc.vector.tensor_copy(out=wb[:], in_=wraw[(e, h)][:].rearrange("p g j n -> p g n j"))
+            elif W_ENGINE[(e, g)] == "scalar":
+                nc.scalar.copy(out=wb[:], in_=src)
             else:
-                nc.scalar.copy(out=wb[:], in_=wraw[(e, h)][:].rearrange("p g j n -> p g n j"))
-            wc[(e, h)] = keep.tile([P, PASSES * NH], U32, name="wc%d_%d" % (e, h), align_bytes=64)
-            ws[(e, h)] = keep.tile([P, PASSES * NH], U8, name="ws%d_%d" % (e, h), align_bytes=64)
+                nc.vector.tensor_copy(out=wb[:], in_=src)
+            wc[(e, g)] = keep.tile([P, N], U32, name="wc%d_%d" % (e, g), align_bytes=64)
+            ws[(e, g)] = keep.tile([P, N], U8, name="ws%d_%d" % (e, g), align_bytes=64)
             nc.vector.quantize_mx(
-                out=wc[(e, h)][:].bitcast(FP8X4),
-                scales=ws[(e, h)][:],
-                in_=wb[:].rearrange("p g n j -> p (g n j)"),
+                out=wc[(e, g)][:].bitcast(FP8X4), scales=ws[(e, g)][:], in_=wb[:].rearrange("p n j -> p (n j)")
             )
 
-        def multiply(e, h):
-            for i in range(NBH):
-                nb = h * NBH + i
+        def multiply(e):
+            for nb in range(NB):
                 acc = psum.tile([P, C], F32, name="acc")
+                cols = slice(nb * P, (nb + 1) * P)
                 for g in range(PASSES):
-                    cols = slice(g * NH + i * P, g * NH + (i + 1) * P)
                     nc.tensor.matmul_mx(
                         out=acc[:],
-                        lhsT=wc[(e, h)][:, cols].bitcast(FP8X4),
-                        lhsT_scale=ws[(e, h)][:, cols],
+                        lhsT=wc[(e, g)][:, cols].bitcast(FP8X4),
+                        lhsT_scale=ws[(e, g)][:, cols],
                         rhs=xc[e][:, g * C : (g + 1) * C].bitcast(FP8X4),
                         rhs_scale=xs[e][:, g * C : (g + 1) * C],
                         start=(g == 0),
@@ -174,27 +160,13 @@ def tile_routed_moe_kernel(tc, xT, w, b, gate, offs, pos1, pos2, out):
 
         for e in range(E):
             x_gather(e)
-        x_words(0)
-        x_words(1)
-        x_quant(0)
-        x_words(2)
-        w_unit(0, 0)
-        x_words(3)
-        x_quant(1)
-        w_unit(1, 0)
-        x_quant(2)
-        w_unit(2, 0)
-        x_quant(3)
-        w_unit(3, 0)
-        w_unit(0, 1)
-        w_unit(1, 1)
-        w_unit(2, 1)
         for e in range(E):
-            multiply(e, 0)
-        w_unit(3, 1)
-        combine(0)
-        combine(1)
+            x_words(e)
         for e in range(E):
-            multiply(e, 1)
-        combine(2)
-        combine(3)
+            x_quant(e)
+        for e in range(E):
+            for g in range(PASSES):
+                w_piece(e, g)
+            multiply(e)
+        for nb in range(NB):
+            combine(nb)

@@ -22,6 +22,7 @@ K_PASS = P * PACK
 PASSES = K // K_PASS
 NB = N // P
 LC = C // 16
+RUN = 4
 UNIT = C * PACK
 S_EXPERTS = (3, 2, 1)
 W_ENGINE = {
@@ -114,17 +115,18 @@ def tile_routed_moe_kernel(tc, xT, w, b, gate, offs, pos1, pos2, out):
 
         def w_piece(e, g):
             wb = keep.tile([P, N, PACK], BF16, name="wb%d_%d" % (e, g), align_bytes=64)
-            src = wraw[(e, g)][:].rearrange("p j n -> p n j")
+            src = wraw[(e, g)][:].rearrange("p j (c i) -> p c j i", i=RUN)
+            dst = wb[:].rearrange("p (c i) j -> p c j i", i=RUN)
             if W_ENGINE[(e, g)] == "gpsimd":
                 for half in range(2):
-                    cols = slice(half * N // 2, (half + 1) * N // 2)
+                    groups = slice(half * N // RUN // 2, (half + 1) * N // RUN // 2)
                     nc.gpsimd.tensor_scalar(
-                        out=wb[:, cols, :], in0=src[:, cols, :], scalar1=1.0, scalar2=0.0, op0=MULT, op1=ADD
+                        out=dst[:, groups], in0=src[:, groups], scalar1=1.0, scalar2=0.0, op0=MULT, op1=ADD
                     )
             elif W_ENGINE[(e, g)] == "scalar":
-                nc.scalar.copy(out=wb[:], in_=src)
+                nc.scalar.copy(out=dst, in_=src)
             else:
-                nc.vector.tensor_copy(out=wb[:], in_=src)
+                nc.vector.tensor_copy(out=dst, in_=src)
             wc[(e, g)] = keep.tile([P, N], U32, name="wc%d_%d" % (e, g), align_bytes=64)
             ws[(e, g)] = keep.tile([P, N], U8, name="ws%d_%d" % (e, g), align_bytes=64)
             nc.vector.quantize_mx(

@@ -1,6 +1,7 @@
 from contextlib import ExitStack
 
 import concourse.mybir as mybir
+from concourse.masks import make_identity
 
 K, T, E, C, N = 1024, 512, 4, 256, 512
 FLOPS = 2 * E * C * K * N
@@ -24,6 +25,7 @@ NB = N // P
 LC = C // 16
 RUN = 4
 UNIT = C * PACK
+PE_SUMS = (0, 1)
 S_EXPERTS = (3, 2, 1)
 W_ENGINE = {
     (0, 0): "gpsimd", (0, 1): "scalar", (1, 0): "gpsimd", (1, 1): "scalar",
@@ -36,8 +38,12 @@ def tile_routed_moe_kernel(tc, xT, w, b, gate, offs, pos1, pos2, out):
     with ExitStack() as ctx:
         lists = ctx.enter_context(tc.tile_pool(name="lists", bufs=1))
         keep = ctx.enter_context(tc.tile_pool(name="keep", bufs=1))
-        comb = ctx.enter_context(tc.tile_pool(name="comb", bufs=2))
-        psum = ctx.enter_context(tc.psum_pool(name="psum", bufs=8))
+        comb = ctx.enter_context(tc.tile_pool(name="comb", bufs=4))
+        psum = ctx.enter_context(tc.psum_pool(name="psum", bufs=6))
+        psum_sum = ctx.enter_context(tc.psum_pool(name="psum_sum", bufs=2))
+
+        ident = keep.tile([P, P], F32, name="ident")
+        make_identity(nc, ident[:])
 
         offs_t = lists.tile([P, E * C // 16], U16, name="offs_t")
         nc.sync.dma_start(offs_t[:], offs)
@@ -115,18 +121,19 @@ def tile_routed_moe_kernel(tc, xT, w, b, gate, offs, pos1, pos2, out):
 
         def w_piece(e, g):
             wb = keep.tile([P, N, PACK], BF16, name="wb%d_%d" % (e, g), align_bytes=64)
-            src = wraw[(e, g)][:].rearrange("p j (c i) -> p c j i", i=RUN)
-            dst = wb[:].rearrange("p (c i) j -> p c j i", i=RUN)
+            src = wraw[(e, g)][:].rearrange("p j n -> p n j")
+            src_runs = wraw[(e, g)][:].rearrange("p j (c i) -> p c j i", i=RUN)
+            dst_runs = wb[:].rearrange("p (c i) j -> p c j i", i=RUN)
             if W_ENGINE[(e, g)] == "gpsimd":
                 for half in range(2):
-                    groups = slice(half * N // RUN // 2, (half + 1) * N // RUN // 2)
+                    cols = slice(half * N // 2, (half + 1) * N // 2)
                     nc.gpsimd.tensor_scalar(
-                        out=dst[:, groups], in0=src[:, groups], scalar1=1.0, scalar2=0.0, op0=MULT, op1=ADD
+                        out=wb[:, cols, :], in0=src[:, cols, :], scalar1=1.0, scalar2=0.0, op0=MULT, op1=ADD
                     )
             elif W_ENGINE[(e, g)] == "scalar":
-                nc.scalar.copy(out=dst, in_=src)
+                nc.scalar.copy(out=dst_runs, in_=src_runs)
             else:
-                nc.vector.tensor_copy(out=dst, in_=src)
+                nc.vector.tensor_copy(out=dst_runs, in_=src_runs)
             wc[(e, g)] = keep.tile([P, N], U32, name="wc%d_%d" % (e, g), align_bytes=64)
             ws[(e, g)] = keep.tile([P, N], U8, name="ws%d_%d" % (e, g), align_bytes=64)
             nc.vector.quantize_mx(
@@ -157,7 +164,13 @@ def tile_routed_moe_kernel(tc, xT, w, b, gate, offs, pos1, pos2, out):
             t2 = comb.tile([P, T], F32, name="t2")
             nc.vector.tensor_tensor(out=t2[:], in0=y[nb][:].indirect(pos2_t[:]), in1=gates[(1, nb)][:], op=MULT)
             res = comb.tile([P, T], F32, name="res")
-            nc.vector.tensor_tensor(out=res[:], in0=t1[:], in1=t2[:], op=ADD)
+            if nb in PE_SUMS:
+                total = psum_sum.tile([P, T], F32, name="total")
+                nc.tensor.matmul(out=total[:], lhsT=ident[:], rhs=t1[:], start=True, stop=False)
+                nc.tensor.matmul(out=total[:], lhsT=ident[:], rhs=t2[:], start=False, stop=True)
+                nc.scalar.copy(out=res[:], in_=total[:])
+            else:
+                nc.vector.tensor_tensor(out=res[:], in0=t1[:], in1=t2[:], op=ADD)
             nc.sync.dma_start(out[nb * P : (nb + 1) * P, :], res[:])
 
         for e in range(E):

@@ -121,19 +121,18 @@ def tile_routed_moe_kernel(tc, xT, w, b, gate, offs, pos1, pos2, out):
 
         def w_piece(e, g):
             wb = keep.tile([P, N, PACK], BF16, name="wb%d_%d" % (e, g), align_bytes=64)
-            src = wraw[(e, g)][:].rearrange("p j n -> p n j")
-            src_runs = wraw[(e, g)][:].rearrange("p j (c i) -> p c j i", i=RUN)
-            dst_runs = wb[:].rearrange("p (c i) j -> p c j i", i=RUN)
+            src = wraw[(e, g)][:].rearrange("p j (c i) -> p c j i", i=RUN)
+            dst = wb[:].rearrange("p (c i) j -> p c j i", i=RUN)
             if W_ENGINE[(e, g)] == "gpsimd":
                 for half in range(2):
-                    cols = slice(half * N // 2, (half + 1) * N // 2)
+                    groups = slice(half * N // RUN // 2, (half + 1) * N // RUN // 2)
                     nc.gpsimd.tensor_scalar(
-                        out=wb[:, cols, :], in0=src[:, cols, :], scalar1=1.0, scalar2=0.0, op0=MULT, op1=ADD
+                        out=dst[:, groups], in0=src[:, groups], scalar1=1.0, scalar2=0.0, op0=MULT, op1=ADD
                     )
             elif W_ENGINE[(e, g)] == "scalar":
-                nc.scalar.copy(out=dst_runs, in_=src_runs)
+                nc.scalar.copy(out=dst, in_=src)
             else:
-                nc.vector.tensor_copy(out=dst_runs, in_=src_runs)
+                nc.vector.tensor_copy(out=dst, in_=src)
             wc[(e, g)] = keep.tile([P, N], U32, name="wc%d_%d" % (e, g), align_bytes=64)
             ws[(e, g)] = keep.tile([P, N], U8, name="ws%d_%d" % (e, g), align_bytes=64)
             nc.vector.quantize_mx(

@@ -29,7 +29,7 @@ PE_SUMS = (0, 1)
 S_EXPERTS = (3, 2, 1)
 W_ENGINE = {
     (0, 0): "gpsimd", (0, 1): "scalar", (1, 0): "gpsimd", (1, 1): "scalar",
-    (2, 0): "gpsimd", (2, 1): "scalar", (3, 0): "scalar", (3, 1): "vector",
+    (2, 0): "vector", (2, 1): "scalar", (3, 0): "scalar", (3, 1): "vector",
 }
 
 

@@ -28,7 +28,7 @@ UNIT = C * PACK
 PE_SUMS = (0, 1)
 S_EXPERTS = (3, 2, 1)
 W_ENGINE = {
-    (0, 0): "gpsimd", (0, 1): "scalar", (1, 0): "gpsimd", (1, 1): "scalar",
+    (0, 0): "gpsimd", (0, 1): "gpsimd", (1, 0): "scalar", (1, 1): "scalar",
     (2, 0): "vector", (2, 1): "scalar", (3, 0): "scalar", (3, 1): "vector",
 }
 
@@ -82,7 +82,9 @@ def tile_routed_moe_kernel(tc, xT, w, b, gate, offs, pos1, pos2, out):
 
         xbf = keep.tile([P, PACK, T], BF16, name="xbf")
         for t in range(PACK):
-            nc.scalar.copy(out=xbf[:, t, :], in_=xr[0][:, t, :])
+            nc.gpsimd.tensor_scalar(
+                out=xbf[:, t, :], in0=xr[0][:, t, :], scalar1=1.0, scalar2=0.0, op0=MULT, op1=ADD
+            )
         for e in S_EXPERTS:
             place = xb[e][:, 0:UNIT].rearrange("p (n t) -> p n t", t=PACK)
             for t in range(PACK):

@@ -29,7 +29,7 @@ PE_SUMS = (0, 1)
 S_EXPERTS = (3, 2, 1)
 W_ENGINE = {
     (0, 0): "gpsimd", (0, 1): "gpsimd", (1, 0): "scalar", (1, 1): "scalar",
-    (2, 0): "vector", (2, 1): "scalar", (3, 0): "scalar", (3, 1): "vector",
+    (2, 0): "scalar", (2, 1): "scalar", (3, 0): "vector", (3, 1): "vector",
 }
 
 
@@ -60,14 +60,19 @@ def tile_routed_moe_kernel(tc, xT, w, b, gate, offs, pos1, pos2, out):
         nc.sync.dma_start(pos2_t[:], pos2)
         b_t = keep.tile([P, NB, E], F32, name="b_t")
 
+        def w_parts(e, g):
+            if (e, g) == (E - 1, PASSES - 1):
+                return [slice(0, N // 2), slice(N // 2, N)]
+            return [slice(0, N)]
+
         wraw = {}
         for e in range(E):
             for g in range(PASSES):
                 wraw[(e, g)] = keep.tile([P, PACK, N], F32, name="raw%d_%d" % (e, g))
-                nc.sync.dma_start(
-                    wraw[(e, g)][:], w[e, g * K_PASS : (g + 1) * K_PASS, :].rearrange("(p j) n -> p j n", j=PACK)
-                )
-                if (e, g) == (3, 0):
+                rows = w[e, g * K_PASS : (g + 1) * K_PASS, :].rearrange("(p j) n -> p j n", j=PACK)
+                for cols in w_parts(e, g):
+                    nc.sync.dma_start(wraw[(e, g)][:, :, cols], rows[:, :, cols])
+                if (e, g) == (2, 1):
                     nc.sync.dma_start(b_t[:], b.rearrange("(nb p) e -> p nb e", p=P))
         gates = {}
         for nb in range(NB):
@@ -123,8 +128,14 @@ def tile_routed_moe_kernel(tc, xT, w, b, gate, offs, pos1, pos2, out):
 
         def w_piece(e, g):
             wb = keep.tile([P, N, PACK], BF16, name="wb%d_%d" % (e, g), align_bytes=64)
-            src = wraw[(e, g)][:].rearrange("p j (c i) -> p c j i", i=RUN)
-            dst = wb[:].rearrange("p (c i) j -> p c j i", i=RUN)
+            wc[(e, g)] = keep.tile([P, N], U32, name="wc%d_%d" % (e, g), align_bytes=64)
+            ws[(e, g)] = keep.tile([P, N], U8, name="ws%d_%d" % (e, g), align_bytes=64)
+            for cols in w_parts(e, g):
+                w_part(e, g, wb, cols)
+
+        def w_part(e, g, wb, cols):
+            src = wraw[(e, g)][:, :, cols].rearrange("p j (c i) -> p c j i", i=RUN)
+            dst = wb[:, cols, :].rearrange("p (c i) j -> p c j i", i=RUN)
             if W_ENGINE[(e, g)] == "gpsimd":
                 for half in range(2):
                     groups = slice(half * N // RUN // 2, (half + 1) * N // RUN // 2)
@@ -135,10 +146,10 @@ def tile_routed_moe_kernel(tc, xT, w, b, gate, offs, pos1, pos2, out):
                 nc.scalar.copy(out=dst, in_=src)
             else:
                 nc.vector.tensor_copy(out=dst, in_=src)
-            wc[(e, g)] = keep.tile([P, N], U32, name="wc%d_%d" % (e, g), align_bytes=64)
-            ws[(e, g)] = keep.tile([P, N], U8, name="ws%d_%d" % (e, g), align_bytes=64)
             nc.vector.quantize_mx(
-                out=wc[(e, g)][:].bitcast(FP8X4), scales=ws[(e, g)][:], in_=wb[:].rearrange("p n j -> p (n j)")
+                out=wc[(e, g)][:, cols].bitcast(FP8X4),
+                scales=ws[(e, g)][:, cols],
+                in_=wb[:, cols, :].rearrange("p n j -> p (n j)"),
             )
 
         def multiply(e):

@@ -25,7 +25,7 @@ NB = N // P
 LC = C // 16
 RUN = 4
 UNIT = C * PACK
-PE_SUMS = (0, 1)
+PE_SUMS = (0, 1, 2)
 S_EXPERTS = (3, 2, 1)
 W_ENGINE = {
     (0, 0): "gpsimd", (0, 1): "gpsimd", (1, 0): "scalar", (1, 1): "scalar",

from contextlib import ExitStack

import concourse.mybir as mybir
from concourse.masks import make_identity

K, T, E, C, N = 1024, 512, 4, 256, 512
FLOPS = 2 * E * C * K * N

F32 = mybir.dt.float32
BF16 = mybir.dt.bfloat16
U32 = mybir.dt.uint32
U16 = mybir.dt.uint16
U8 = mybir.dt.uint8
FP8X4 = mybir.dt.float8_e4m3fn_x4
MULT = mybir.AluOpType.mult
ADD = mybir.AluOpType.add
RELU = mybir.ActivationFunctionType.Relu
COPY = mybir.ActivationFunctionType.Copy

P = 128
PACK = 4
K_PASS = P * PACK
PASSES = K // K_PASS
NB = N // P
LC = C // 16
RUN = 4
UNIT = C * PACK
PE_SUMS = (0, 1, 2)
S_EXPERTS = (3, 2, 1)
W_ENGINE = {
    (0, 0): "gpsimd", (0, 1): "gpsimd", (1, 0): "scalar", (1, 1): "scalar",
    (2, 0): "scalar", (2, 1): "scalar", (3, 0): "vector", (3, 1): "vector",
}


def tile_routed_moe_kernel(tc, xT, w, b, gate, offs, pos1, pos2, out):
    nc = tc.nc
    with ExitStack() as ctx:
        lists = ctx.enter_context(tc.tile_pool(name="lists", bufs=1))
        keep = ctx.enter_context(tc.tile_pool(name="keep", bufs=1))
        comb = ctx.enter_context(tc.tile_pool(name="comb", bufs=4))
        psum = ctx.enter_context(tc.psum_pool(name="psum", bufs=6))
        psum_sum = ctx.enter_context(tc.psum_pool(name="psum_sum", bufs=2))

        ident = keep.tile([P, P], F32, name="ident")
        make_identity(nc, ident[:])

        offs_t = lists.tile([P, E * C // 16], U16, name="offs_t")
        nc.sync.dma_start(offs_t[:], offs)

        x_view = xT.rearrange("(g p t) n -> g p t n", p=P, t=PACK)
        xr = [keep.tile([P, PACK, T], F32, name="xr%d" % g) for g in range(PASSES)]
        for g in range(PASSES):
            for t in range(PACK):
                nc.sync.dma_start(xr[g][:, t, :], x_view[g, :, t, :])

        pos1_t = lists.tile([P, T // 16], U16, name="pos1_t")
        nc.sync.dma_start(pos1_t[:], pos1)
        pos2_t = lists.tile([P, T // 16], U16, name="pos2_t")
        nc.sync.dma_start(pos2_t[:], pos2)
        b_t = keep.tile([P, NB, E], F32, name="b_t")

        def w_parts(e, g):
            if (e, g) == (E - 1, PASSES - 1):
                return [slice(0, N // 2), slice(N // 2, N)]
            return [slice(0, N)]

        wraw = {}
        for e in range(E):
            for g in range(PASSES):
                wraw[(e, g)] = keep.tile([P, PACK, N], F32, name="raw%d_%d" % (e, g))
                rows = w[e, g * K_PASS : (g + 1) * K_PASS, :].rearrange("(p j) n -> p j n", j=PACK)
                for cols in w_parts(e, g):
                    nc.sync.dma_start(wraw[(e, g)][:, :, cols], rows[:, :, cols])
                if (e, g) == (2, 1):
                    nc.sync.dma_start(b_t[:], b.rearrange("(nb p) e -> p nb e", p=P))
        gates = {}
        for nb in range(NB):
            for r in range(2):
                gates[(r, nb)] = keep.tile([P, T], F32, name="gate%d_%d" % (r, nb))
                nc.sync.dma_start(gates[(r, nb)][:], gate[r, nb * P : (nb + 1) * P, :])

        y = [keep.tile([P, E * C], F32, name="y%d" % nb) for nb in range(NB)]
        pr, xb, xc, xs, wc, ws = {}, {}, {}, {}, {}, {}
        for e in range(E):
            xb[e] = keep.tile([P, PASSES * UNIT], BF16, name="xb%d" % e, align_bytes=64)

        xbf = keep.tile([P, PACK, T], BF16, name="xbf")
        for t in range(PACK):
            nc.gpsimd.tensor_scalar(
                out=xbf[:, t, :], in0=xr[0][:, t, :], scalar1=1.0, scalar2=0.0, op0=MULT, op1=ADD
            )
        for e in S_EXPERTS:
            place = xb[e][:, 0:UNIT].rearrange("p (n t) -> p n t", t=PACK)
            for t in range(PACK):
                nc.scalar.activation(
                    out=place[:, :, t],
                    in_=xbf[:, t, :].indirect(offs_t[:, e * LC : (e + 1) * LC]),
                    func=COPY,
                )

        def v_passes(e):
            return [g for g in range(PASSES) if not (g == 0 and e in S_EXPERTS)]

        def x_gather(e):
            gs = v_passes(e)
            pr[e] = keep.tile([P, len(gs) * UNIT], BF16, name="pr%d" % e, align_bytes=64)
            view = pr[e][:].rearrange("p (a u n i) -> p a u n i", a=len(gs), u=2, i=2)
            for a, g in enumerate(gs):
                for t in range(PACK):
                    nc.vector.tensor_copy(
                        out=view[:, a, t // 2, :, t % 2],
                        in_=xr[g][:, t, :].indirect(offs_t[:, e * LC : (e + 1) * LC]),
                    )

        def x_words(e):
            gs = v_passes(e)
            first = gs[0] * UNIT // 2
            nc.vector.tensor_copy(
                out=xb[e][:].bitcast(F32)[:, first:].rearrange("p (a n u) -> p a n u", a=len(gs), u=2),
                in_=pr[e][:].bitcast(F32).rearrange("p (a u n) -> p a n u", a=len(gs), u=2),
            )

        def x_quant(e):
            xc[e] = keep.tile([P, PASSES * C], U32, name="xc%d" % e, align_bytes=64)
            xs[e] = keep.tile([P, PASSES * C], U8, name="xs%d" % e, align_bytes=64)
            nc.vector.quantize_mx(out=xc[e][:].bitcast(FP8X4), scales=xs[e][:], in_=xb[e][:])

        def w_piece(e, g):
            wb = keep.tile([P, N, PACK], BF16, name="wb%d_%d" % (e, g), align_bytes=64)
            wc[(e, g)] = keep.tile([P, N], U32, name="wc%d_%d" % (e, g), align_bytes=64)
            ws[(e, g)] = keep.tile([P, N], U8, name="ws%d_%d" % (e, g), align_bytes=64)
            for cols in w_parts(e, g):
                w_part(e, g, wb, cols)

        def w_part(e, g, wb, cols):
            src = wraw[(e, g)][:, :, cols].rearrange("p j (c i) -> p c j i", i=RUN)
            dst = wb[:, cols, :].rearrange("p (c i) j -> p c j i", i=RUN)
            if W_ENGINE[(e, g)] == "gpsimd":
                for half in range(2):
                    groups = slice(half * N // RUN // 2, (half + 1) * N // RUN // 2)
                    nc.gpsimd.tensor_scalar(
                        out=dst[:, groups], in0=src[:, groups], scalar1=1.0, scalar2=0.0, op0=MULT, op1=ADD
                    )
            elif W_ENGINE[(e, g)] == "scalar":
                nc.scalar.copy(out=dst, in_=src)
            else:
                nc.vector.tensor_copy(out=dst, in_=src)
            nc.vector.quantize_mx(
                out=wc[(e, g)][:, cols].bitcast(FP8X4),
                scales=ws[(e, g)][:, cols],
                in_=wb[:, cols, :].rearrange("p n j -> p (n j)"),
            )

        def multiply(e):
            for nb in range(NB):
                acc = psum.tile([P, C], F32, name="acc")
                cols = slice(nb * P, (nb + 1) * P)
                for g in range(PASSES):
                    nc.tensor.matmul_mx(
                        out=acc[:],
                        lhsT=wc[(e, g)][:, cols].bitcast(FP8X4),
                        lhsT_scale=ws[(e, g)][:, cols],
                        rhs=xc[e][:, g * C : (g + 1) * C].bitcast(FP8X4),
                        rhs_scale=xs[e][:, g * C : (g + 1) * C],
                        start=(g == 0),
                        stop=(g == PASSES - 1),
                    )
                nc.scalar.activation(
                    out=y[nb][:, e * C : (e + 1) * C], in_=acc[:], func=RELU, bias=b_t[:, nb, e : e + 1]
                )

        def combine(nb):
            t1 = comb.tile([P, T], F32, name="t1")
            nc.vector.tensor_tensor(out=t1[:], in0=y[nb][:].indirect(pos1_t[:]), in1=gates[(0, nb)][:], op=MULT)
            t2 = comb.tile([P, T], F32, name="t2")
            nc.vector.tensor_tensor(out=t2[:], in0=y[nb][:].indirect(pos2_t[:]), in1=gates[(1, nb)][:], op=MULT)
            res = comb.tile([P, T], F32, name="res")
            if nb in PE_SUMS:
                total = psum_sum.tile([P, T], F32, name="total")
                nc.tensor.matmul(out=total[:], lhsT=ident[:], rhs=t1[:], start=True, stop=False)
                nc.tensor.matmul(out=total[:], lhsT=ident[:], rhs=t2[:], start=False, stop=True)
                nc.scalar.copy(out=res[:], in_=total[:])
            else:
                nc.vector.tensor_tensor(out=res[:], in0=t1[:], in1=t2[:], op=ADD)
            nc.sync.dma_start(out[nb * P : (nb + 1) * P, :], res[:])

        for e in range(E):
            x_gather(e)
        for e in range(E):
            x_words(e)
        for e in range(E):
            x_quant(e)
        for e in range(E):
            for g in range(PASSES):
                w_piece(e, g)
            multiply(e)
        for nb in range(NB):
            combine(nb)
